import numpy as np
import ml_dtypes


def mxq(x, axis, fmt="e4m3"):
    dtype, down = {"e4m3": (ml_dtypes.float8_e4m3fn, 7), "e5m2": (ml_dtypes.float8_e5m2, 14)}[fmt]
    v = np.moveaxis(np.asarray(x, np.float32).astype(ml_dtypes.bfloat16).astype(np.float64), axis, -1)
    blocks = v.reshape(v.shape[:-1] + (-1, 32))
    amax = np.abs(blocks).max(-1, keepdims=True)
    byte = np.maximum(np.where(amax > 0, np.frexp(amax)[1] - 1 + 127, 0) - down, 1)
    scale = np.exp2(byte - 127.0)
    codes = (blocks / scale).astype(np.float32).astype(dtype).astype(np.float64)
    return np.moveaxis((codes * scale).reshape(v.shape), -1, axis)


WIDE = False


def mx_kscale(k):
    if not WIDE:
        return np.ones(k)
    levels = np.array([10, -10, 5, -5, 0])
    if k % 512:
        return np.exp2(np.random.permutation(np.resize(levels, k // 32))).repeat(32)
    a = np.empty((k // 512, 16))
    for p in range(k // 512):
        a[p, :8] = np.random.permutation(np.resize(levels, 8))
        for g in range(8):
            far = levels[np.abs(levels - a[p, g]) >= 10]
            a[p, g + 8] = far[np.random.randint(len(far))]
    return np.exp2(a.ravel()).repeat(32)


def f64(x):
    return np.asarray(x).astype(np.float64)


def striped(idx):
    return np.tile(np.asarray(idx).reshape(-1, 16).T, (8, 1)).astype(np.uint16)


def unstriped(offs):
    return offs[:16].T.reshape(-1).astype(np.int64)


E2M1 = np.array([0.0, 0.5, 1.0, 1.5, 2.0, 3.0, 4.0, 6.0, -0.0, -0.5, -1.0, -1.5, -2.0, -3.0, -4.0, -6.0])


def pack_weight(w, fmt):
    k, n = w.shape
    w = f64(np.asarray(w, np.float32).astype(ml_dtypes.bfloat16)).reshape(k // 32, 32, n)
    amax = np.abs(w).max(1)
    if fmt == "e4m3":
        byte = np.frexp(amax)[1] - 1 + 127 - 7
    else:
        mant, ex = np.frexp(amax / 6.0)
        byte = np.where(mant > 0.5, ex, ex - 1) + 127
    byte = np.clip(np.where(amax > 0, byte, 1), 1, 254)
    scaled = (w * np.exp2(127.0 - byte)[:, None, :]).reshape(k, n).astype(np.float32)
    by_word = np.ascontiguousarray(scaled.reshape(k // 512, 128, 4, n).transpose(0, 1, 3, 2))
    if fmt == "e4m3":
        words = by_word.astype(ml_dtypes.float8_e4m3fn).view(np.uint8)
    else:
        c = by_word.astype(ml_dtypes.float4_e2m1fn).view(np.uint8) & 0xF
        words = (c[..., 0::2] | (c[..., 1::2] << 4)).reshape(k // 512, 128, 2 * n)
    return np.ascontiguousarray(words), np.ascontiguousarray(byte.astype(np.uint8).reshape(k // 512, 16, n))


def unpack_weight(words, scales, fmt):
    g, _, n = scales.shape
    words = np.ascontiguousarray(words).reshape(g, 128, n, -1)
    if fmt == "e4m3":
        vals = words.view(ml_dtypes.float8_e4m3fn).astype(np.float64)
    else:
        nib = np.empty((g, 128, n, 4), np.uint8)
        nib[..., 0::2] = words & 0xF
        nib[..., 1::2] = words >> 4
        vals = E2M1[nib]
    vals = vals * np.repeat(np.exp2(scales.astype(np.float64) - 127.0), 8, axis=1)[..., None]
    return vals.transpose(0, 1, 3, 2).reshape(g * 512, n)


D, E, T, I, Q = 512, 512, 2048, 512, 128


def setup_inputs():
    n = np.random.standard_normal
    idx = np.random.permutation(T)[:I]
    fd = mx_kscale(D)
    fi = mx_kscale(I)
    ti = np.ones(T)
    ti[idx] = fi
    keysp = pack_weight(n((D, T)) / fd[:, None], "e2m1")
    return {
        "query": (n((D, Q)) * 1.0 / np.sqrt(D) * fd[:, None]).astype(np.float32),
        "keys_words": keysp[0],
        "keys_scales": keysp[1],
        "aim": (np.random.uniform(0.5, 2.0, (Q, 1))).astype(np.float32),
        "soft": (np.random.uniform(0.5, 2.0, (Q, 1))).astype(np.float32),
        "dquery": (n((D, Q)) * 0.6 / np.sqrt(D) * fd[:, None]).astype(np.float32),
        "os": (np.random.uniform(4.0, 16.0, (1, I)) * fi).astype(np.float32),
        "vals": (n((E, T)) / ti).astype(np.float32),
        "offs": striped(idx),
    }


def reference(query, keys_words, keys_scales, aim, soft, dquery, os, vals, offs):
    idx = unstriped(offs)
    keysu = unpack_weight(keys_words, keys_scales, "e2m1")
    queryq = mxq(f64(query), 0, "e4m3")
    keysidxg = keysu[:, idx]
    a = queryq.T @ keysidxg
    dqueryq = mxq(f64(dquery), 0, "e4m3")
    ta = dqueryq.T @ keysidxg
    p = 1.0 / (np.square(f64(aim) - a) + f64(soft))
    z = np.sum(p, axis=1, keepdims=True)
    tp = ta * (-1.0) * (f64(aim) - a) * 2.0 * (-1.0) / np.square(np.square(f64(aim) - a) + f64(soft))
    tz = np.sum(tp, axis=1, keepdims=True)
    tw = (tp - tz * p / z) / z
    wo1 = tw * f64(os)
    wt1 = wo1.T
    vt1 = f64(vals)[:, idx].T
    wt1q = mxq(wt1, 0, "e4m3")
    vt1q = mxq(vt1, 0, "e4m3")
    o = wt1q.T @ vt1q
    return o

@@ -1,0 +1,174 @@
+from contextlib import ExitStack
+
+import concourse.mybir as mybir
+from concourse.masks import make_identity
+
+D, E, T, I, Q = 512, 512, 2048, 512, 128
+FLOPS = 2 * (2 * D * Q * I + I * Q * E)
+
+F32 = mybir.dt.float32
+BF16 = mybir.dt.bfloat16
+I32 = mybir.dt.int32
+U32 = mybir.dt.uint32
+U16 = mybir.dt.uint16
+U8 = mybir.dt.uint8
+FP8X4 = mybir.dt.float8_e4m3fn_x4
+FP4X4 = mybir.dt.float4_e2m1fn_x4
+ACT = mybir.ActivationFunctionType
+ALU = mybir.AluOpType
+
+P = 128
+PACK = 4
+BLOCKS = E // P
+
+
+def tile_attend_ttnearpoint_kernel(tc, query, keys_words, keys_scales, aim, soft, dquery, slot_factor, vals, offs, out):
+    nc = tc.nc
+    with ExitStack() as ctx:
+        sb = ctx.enter_context(tc.tile_pool(name="sb", bufs=1))
+        ps = ctx.enter_context(tc.psum_pool(name="ps", bufs=1))
+
+        offsets = sb.tile([P, I // 16], U16, name="offsets")
+        nc.sync.dma_start(offsets[:], offs)
+
+        key_scales = sb.tile([P, T], U8, name="key_scales", align_bytes=64)
+        nc.vector.memset(key_scales[:].bitcast(I32), 0)
+        for quadrant in range(4):
+            nc.sync.dma_start(
+                key_scales[32 * quadrant : 32 * quadrant + 4, :].bitcast(I32),
+                keys_scales[0, 4 * quadrant : 4 * quadrant + 4, :].bitcast(I32),
+            )
+        query_raw = sb.tile([P, PACK, Q], F32, name="query_raw")
+        nc.sync.dma_start(query_raw[:], query.rearrange("(p t) q -> p t q", t=PACK))
+        key_words = sb.tile([P, T], U16, name="key_words", align_bytes=64)
+        nc.sync.dma_start(key_words[:].bitcast(I32), keys_words[0].bitcast(I32))
+        dquery_raw = sb.tile([P, PACK, Q], F32, name="dquery_raw")
+        nc.sync.dma_start(dquery_raw[:], dquery.rearrange("(p t) q -> p t q", t=PACK))
+        aim_col = sb.tile([P, 1], F32, name="aim_col")
+        soft_col = sb.tile([P, 1], F32, name="soft_col")
+        factor_cols = sb.tile([P, PACK], F32, name="factor_cols")
+        nc.sync.dma_start(aim_col[:], aim)
+        nc.sync.dma_start(soft_col[:], soft)
+        nc.sync.dma_start(factor_cols[:], slot_factor.rearrange("o (p t) -> (o p) t", t=PACK))
+        val_pools = []
+        for j in range(BLOCKS):
+            val_pool = sb.tile([P, T], F32, name="val_pool%d" % j)
+            nc.sync.dma_start(val_pool[:], vals[j * P : (j + 1) * P, :])
+            val_pools.append(val_pool)
+
+        identity = sb.tile([P, P], F32, name="identity")
+        make_identity(nc, identity[:])
+
+        warm_in = sb.tile([P, 1], F32, name="warm_in")
+        warm_out = sb.tile([P, 1], F32, name="warm_out")
+        nc.vector.memset(warm_in[:], 1.0)
+        nc.scalar.activation(warm_out[:], warm_in[:], ACT.Abs_reciprocal_sqrt)
+
+        def quantize(name, grouped, width):
+            codes = sb.tile([P, width], U32, name=name + "_codes", align_bytes=64)
+            scales = sb.tile([P, width], U8, name=name + "_scales", align_bytes=64)
+            nc.vector.quantize_mx(out=codes[:].bitcast(FP8X4), scales=scales[:], in_=grouped)
+            return codes, scales
+
+        picked_scales = sb.tile([P, I], U8, name="picked_scales", align_bytes=64)
+        picked_words = sb.tile([P, I], U16, name="picked_words", align_bytes=64)
+        query_grouped = sb.tile([P, Q, PACK], BF16, name="query_grouped", align_bytes=64)
+        dquery_grouped = sb.tile([P, Q, PACK], BF16, name="dquery_grouped", align_bytes=64)
+        nc.vector.tensor_copy(picked_scales[:], key_scales[:].indirect(offsets[:]))
+        nc.scalar.copy(query_grouped[:], query_raw[:].rearrange("p t q -> p q t"))
+        query_codes, query_scales = quantize("query", query_grouped[:].rearrange("p q t -> p (q t)"), Q)
+        nc.vector.tensor_copy(picked_words[:], key_words[:].indirect(offsets[:]))
+        nc.scalar.copy(dquery_grouped[:], dquery_raw[:].rearrange("p t q -> p q t"))
+        dquery_codes, dquery_scales = quantize("dquery", dquery_grouped[:].rearrange("p q t -> p (q t)"), Q)
+
+        score = ps.tile([P, I], F32, name="score")
+        dscore = ps.tile([P, I], F32, name="dscore")
+        for acc, codes, scales in ((score, query_codes, query_scales), (dscore, dquery_codes, dquery_scales)):
+            nc.tensor.matmul_mx(
+                out=acc[:],
+                lhsT=codes[:].bitcast(FP8X4),
+                lhsT_scale=scales[:],
+                rhs=picked_words[:].bitcast(FP4X4),
+                rhs_scale=picked_scales[:],
+                start=True,
+                stop=True,
+            )
+
+        def gather_values(j):
+            picked = sb.tile([P, I], BF16, name="picked_vals%d" % j, align_bytes=64)
+            nc.vector.tensor_copy(picked[:], val_pools[j][:].indirect(offsets[:]))
+            pairs = picked[:].bitcast(F32)
+            turned = ps.tile([P, 2, P], F32, name="turned_vals%d" % (j % 3))
+            for u in range(2):
+                nc.tensor.transpose(turned[:, u, :], pairs[:, u::2], identity[:])
+            grouped = sb.tile([P, P * PACK], BF16, name="vals_grouped%d" % j, align_bytes=64)
+            nc.scalar.copy(
+                grouped[:].bitcast(F32).rearrange("p (e u) -> p e u", u=2),
+                turned[:].rearrange("p u e -> p e u"),
+            )
+            return grouped
+
+        def wide(name):
+            return sb.tile([P, PACK, P], F32, name=name)
+
+        def col(name):
+            return sb.tile([P, 1], F32, name=name)
+
+        def flat(t):
+            return t[:].rearrange("q t s -> q (t s)")
+
+        score_dealt = score[:].rearrange("q (s t) -> q t s", t=PACK)
+        dscore_dealt = dscore[:].rearrange("q (s t) -> q t s", t=PACK)
+        gap_sq, gap, root, part, part_sq, weight = [wide(n) for n in ("gap_sq", "gap", "root", "part", "part_sq", "weight")]
+        slope, dpart, dweight = [wide(n) for n in ("slope", "dpart", "dweight")]
+        z, rz, c = col("z"), col("rz"), col("c")
+
+        grouped_vals = [gather_values(0)]
+        nc.scalar.activation(gap_sq[:], score_dealt, ACT.Square, bias=aim_col[:], scale=-1.0)
+        nc.scalar.activation(gap[:], score_dealt, ACT.Identity, bias=aim_col[:], scale=-1.0)
+        nc.scalar.activation(flat(root), flat(gap_sq), ACT.Abs_reciprocal_sqrt, bias=soft_col[:])
+        nc.vector.scalar_tensor_tensor(slope[:], gap[:], -2.0, dscore_dealt, ALU.mult, ALU.mult)
+        nc.scalar.activation(flat(part), flat(root), ACT.Square, accum_out=z[:])
+        nc.vector.reciprocal(rz[:], z[:])
+        nc.scalar.activation(flat(part_sq), flat(part), ACT.Square)
+        nc.scalar.activation(flat(weight), flat(part), ACT.Copy, scale=rz[:])
+        quantized_vals = [quantize("vals0", grouped_vals[0][:], P)]
+        grouped_vals.append(gather_values(1))
+        nc.vector.scalar_tensor_tensor(flat(dpart), flat(slope), rz[:], flat(part_sq), ALU.mult, ALU.mult, accum_out=c[:])
+        nc.vector.scalar_tensor_tensor(flat(dweight), flat(weight), c[:], flat(dpart), ALU.mult, ALU.subtract)
+        quantized_vals.append(quantize("vals1", grouped_vals[1][:], P))
+        turned_w = ps.tile([P, PACK, Q], F32, name="turned_w")
+        for t in range(PACK):
+            nc.tensor.transpose(turned_w[:, t, :], dweight[:, t, :], identity[:])
+        grouped_vals.append(gather_values(2))
+        w_grouped = sb.tile([P, Q, PACK], BF16, name="w_grouped", align_bytes=64)
+        nc.vector.tensor_tensor(
+            w_grouped[:],
+            turned_w[:].rearrange("p t q -> p q t"),
+            factor_cols[:].unsqueeze(1).to_broadcast([P, Q, PACK]),
+            ALU.mult,
+        )
+        quantized_vals.append(quantize("vals2", grouped_vals[2][:], P))
+        w_codes, w_scales = quantize("w", w_grouped[:].rearrange("p q t -> p (q t)"), Q)
+        grouped_vals.append(gather_values(3))
+        quantized_vals.append(quantize("vals3", grouped_vals[3][:], P))
+
+        early = ps.tile([P, (BLOCKS - 1) * P], F32, name="early")
+        late = ps.tile([P, P], F32, name="late")
+        for j in range(BLOCKS):
+            codes, scales = quantized_vals[j]
+            nc.tensor.matmul_mx(
+                out=early[:, j * P : (j + 1) * P] if j < BLOCKS - 1 else late[:],
+                lhsT=w_codes[:].bitcast(FP8X4),
+                lhsT_scale=w_scales[:],
+                rhs=codes[:].bitcast(FP8X4),
+                rhs_scale=scales[:],
+                start=True,
+                stop=True,
+            )
+        early_out = sb.tile([P, (BLOCKS - 1) * P], F32, name="early_out")
+        late_out = sb.tile([P, P], F32, name="late_out")
+        nc.scalar.copy(early_out[:], early[:])
+        nc.sync.dma_start(out[:, : (BLOCKS - 1) * P], early_out[:])
+        nc.vector.tensor_copy(late_out[:], late[:])
+        nc.sync.dma_start(out[:, (BLOCKS - 1) * P :], late_out[:])

@@ -31,144 +31,172 @@ def tile_attend_ttnearpoint_kernel(tc, query, keys_words, keys_scales, aim, soft
         offsets = sb.tile([P, I // 16], U16, name="offsets")
         nc.sync.dma_start(offsets[:], offs)
 
-        key_scales = sb.tile([P, T], U8, name="key_scales", align_bytes=64)
-        nc.vector.memset(key_scales[:].bitcast(I32), 0)
-        for quadrant in range(4):
-            nc.sync.dma_start(
-                key_scales[32 * quadrant : 32 * quadrant + 4, :].bitcast(I32),
-                keys_scales[0, 4 * quadrant : 4 * quadrant + 4, :].bitcast(I32),
-            )
-        query_raw = sb.tile([P, PACK, Q], F32, name="query_raw")
-        nc.sync.dma_start(query_raw[:], query.rearrange("(p t) q -> p t q", t=PACK))
-        key_words = sb.tile([P, T], U16, name="key_words", align_bytes=64)
+        key_words = sb.tile([P, T], U16, name="key_words", tag="key_words", align_bytes=64)
         nc.sync.dma_start(key_words[:].bitcast(I32), keys_words[0].bitcast(I32))
-        dquery_raw = sb.tile([P, PACK, Q], F32, name="dquery_raw")
+        query_raw = sb.tile([P, PACK, Q], F32, name="query_raw", tag="query_raw", align_bytes=64)
+        nc.sync.dma_start(query_raw[:], query.rearrange("(p t) q -> p t q", t=PACK))
+        key_scales = sb.tile([P, T], U8, name="key_scales", tag="key_scales", align_bytes=64)
+        nc.gpsimd.memset(key_scales[:, : T // 2].bitcast(I32), 0)
+        nc.vector.memset(key_scales[:, T // 2 :].bitcast(I32), 0)
+        for r in range(4):
+            nc.sync.dma_start(key_scales[r:P:32, :].bitcast(I32), keys_scales[0, r:16:4, :].bitcast(I32))
+        dquery_raw = sb.tile([P, PACK, Q], F32, name="dquery_raw", tag="dquery_raw", align_bytes=64)
         nc.sync.dma_start(dquery_raw[:], dquery.rearrange("(p t) q -> p t q", t=PACK))
-        aim_col = sb.tile([P, 1], F32, name="aim_col")
-        soft_col = sb.tile([P, 1], F32, name="soft_col")
-        factor_cols = sb.tile([P, PACK], F32, name="factor_cols")
-        nc.sync.dma_start(aim_col[:], aim)
-        nc.sync.dma_start(soft_col[:], soft)
-        nc.sync.dma_start(factor_cols[:], slot_factor.rearrange("o (p t) -> (o p) t", t=PACK))
-        val_pools = []
-        for j in range(BLOCKS):
-            val_pool = sb.tile([P, T], F32, name="val_pool%d" % j)
-            nc.sync.dma_start(val_pool[:], vals[j * P : (j + 1) * P, :])
-            val_pools.append(val_pool)
 
-        identity = sb.tile([P, P], F32, name="identity")
-        make_identity(nc, identity[:])
-
-        warm_in = sb.tile([P, 1], F32, name="warm_in")
+        warm_in = sb.tile([P, 1], F32, name="warm_in", tag="warm_in", align_bytes=64)
         warm_out = sb.tile([P, 1], F32, name="warm_out")
         nc.vector.memset(warm_in[:], 1.0)
         nc.scalar.activation(warm_out[:], warm_in[:], ACT.Abs_reciprocal_sqrt)
 
-        def quantize(name, grouped, width):
-            codes = sb.tile([P, width], U32, name=name + "_codes", align_bytes=64)
+        aim_col = sb.tile([P, 1], F32, name="aim_col")
+        soft_col = sb.tile([P, 1], F32, name="soft_col")
+        factor_cols = sb.tile([P, PACK], F32, name="factor_cols", tag="factor_cols", align_bytes=64)
+        nc.gpsimd.dma_start(aim_col[:], aim)
+        nc.gpsimd.dma_start(soft_col[:], soft)
+        nc.gpsimd.dma_start(factor_cols[:], slot_factor.rearrange("o (p t) -> (o p) t", t=PACK))
+        identity = sb.tile([P, P], F32, name="identity")
+        make_identity(nc, identity[:])
+
+        pool_tags = ("warm_in", "key_words", "key_scales", "warm_in")
+
+        def load_values(j):
+            val_pool = sb.tile([P, T], F32, name="val_pool%d" % j, tag=pool_tags[j], align_bytes=64)
+            nc.sync.dma_start(val_pool[:], vals[j * P : (j + 1) * P, :])
+            return val_pool
+
+        def quantize(name, grouped, width, tag=""):
+            codes = sb.tile([P, width], U32, name=name + "_codes", tag=tag, align_bytes=64)
             scales = sb.tile([P, width], U8, name=name + "_scales", align_bytes=64)
             nc.vector.quantize_mx(out=codes[:].bitcast(FP8X4), scales=scales[:], in_=grouped)
             return codes, scales
 
         picked_scales = sb.tile([P, I], U8, name="picked_scales", align_bytes=64)
         picked_words = sb.tile([P, I], U16, name="picked_words", align_bytes=64)
-        query_grouped = sb.tile([P, Q, PACK], BF16, name="query_grouped", align_bytes=64)
-        dquery_grouped = sb.tile([P, Q, PACK], BF16, name="dquery_grouped", align_bytes=64)
-        nc.vector.tensor_copy(picked_scales[:], key_scales[:].indirect(offsets[:]))
-        nc.scalar.copy(query_grouped[:], query_raw[:].rearrange("p t q -> p q t"))
-        query_codes, query_scales = quantize("query", query_grouped[:].rearrange("p q t -> p (q t)"), Q)
+        rows_grouped = sb.tile([P, 2 * Q * PACK], BF16, name="rows_grouped", tag="rows_grouped", align_bytes=64)
         nc.vector.tensor_copy(picked_words[:], key_words[:].indirect(offsets[:]))
-        nc.scalar.copy(dquery_grouped[:], dquery_raw[:].rearrange("p t q -> p q t"))
-        dquery_codes, dquery_scales = quantize("dquery", dquery_grouped[:].rearrange("p q t -> p (q t)"), Q)
+        nc.vector.tensor_copy(picked_scales[:], key_scales[:].indirect(offsets[:]))
+        for n, raw in enumerate((query_raw, dquery_raw)):
+            nc.scalar.copy(
+                rows_grouped[:, n * Q * PACK : (n + 1) * Q * PACK].rearrange("p (q t) -> p q t", t=PACK),
+                raw[:].rearrange("p t q -> p q t"),
+            )
+        val_pools = [load_values(j) for j in range(BLOCKS - 1)]
+        rows_codes, rows_scales = quantize("rows", rows_grouped[:], 2 * Q)
 
-        score = ps.tile([P, I], F32, name="score")
+        score = ps.tile([P, I], F32, name="score", tag="score")
         dscore = ps.tile([P, I], F32, name="dscore")
-        for acc, codes, scales in ((score, query_codes, query_scales), (dscore, dquery_codes, dquery_scales)):
+        for n, acc in enumerate((score, dscore)):
             nc.tensor.matmul_mx(
                 out=acc[:],
-                lhsT=codes[:].bitcast(FP8X4),
-                lhsT_scale=scales[:],
+                lhsT=rows_codes[:, n * Q : (n + 1) * Q].bitcast(FP8X4),
+                lhsT_scale=rows_scales[:, n * Q : (n + 1) * Q],
                 rhs=picked_words[:].bitcast(FP4X4),
                 rhs_scale=picked_scales[:],
                 start=True,
                 stop=True,
             )
 
-        def gather_values(j):
-            picked = sb.tile([P, I], BF16, name="picked_vals%d" % j, align_bytes=64)
+        def gather_values(j, tag, bank):
+            picked = sb.tile([P, I], BF16, name="picked_vals%d" % j, tag=tag, align_bytes=64)
             nc.vector.tensor_copy(picked[:], val_pools[j][:].indirect(offsets[:]))
             pairs = picked[:].bitcast(F32)
-            turned = ps.tile([P, 2, P], F32, name="turned_vals%d" % (j % 3))
+            turned = ps.tile([P, 2, P], F32, name="turned_vals%d" % j, tag=bank)
             for u in range(2):
                 nc.tensor.transpose(turned[:, u, :], pairs[:, u::2], identity[:])
-            grouped = sb.tile([P, P * PACK], BF16, name="vals_grouped%d" % j, align_bytes=64)
+            return turned
+
+        def grouped_tile(name, blocks, tag):
+            return sb.tile([P, blocks * P * PACK], BF16, name=name, tag=tag, align_bytes=64)
+
+        def group_values(grouped, turned):
             nc.scalar.copy(
-                grouped[:].bitcast(F32).rearrange("p (e u) -> p e u", u=2),
+                grouped.bitcast(F32).rearrange("p (e u) -> p e u", u=2),
                 turned[:].rearrange("p u e -> p e u"),
             )
-            return grouped
 
-        def wide(name):
-            return sb.tile([P, PACK, P], F32, name=name)
+        def wide(name, tag=""):
+            return sb.tile([P, PACK, P], F32, name=name, tag=tag or name, align_bytes=64)
 
         def col(name):
-            return sb.tile([P, 1], F32, name=name)
+            return sb.tile([P, 1], F32, name=name, tag=name, align_bytes=64)
 
         def flat(t):
             return t[:].rearrange("q t s -> q (t s)")
 
         score_dealt = score[:].rearrange("q (s t) -> q t s", t=PACK)
         dscore_dealt = dscore[:].rearrange("q (s t) -> q t s", t=PACK)
-        gap_sq, gap, root, part, part_sq, weight = [wide(n) for n in ("gap_sq", "gap", "root", "part", "part_sq", "weight")]
-        slope, dpart, dweight = [wide(n) for n in ("slope", "dpart", "dweight")]
-        z, rz, c = col("z"), col("rz"), col("c")
+        gap_sq, gap, root, part, weight, shift, slope, dpart = [
+            wide(n) for n in ("gap_sq", "gap", "root", "part", "weight", "shift", "slope", "dpart")
+        ]
+        z, nz, nrz, c = col("z"), col("nz"), col("nrz"), col("c")
 
-        grouped_vals = [gather_values(0)]
+        turned0 = gather_values(0, "rows_grouped", "bank0")
+        val_pools.append(load_values(3))
         nc.scalar.activation(gap_sq[:], score_dealt, ACT.Square, bias=aim_col[:], scale=-1.0)
         nc.scalar.activation(gap[:], score_dealt, ACT.Identity, bias=aim_col[:], scale=-1.0)
         nc.scalar.activation(flat(root), flat(gap_sq), ACT.Abs_reciprocal_sqrt, bias=soft_col[:])
         nc.vector.scalar_tensor_tensor(slope[:], gap[:], -2.0, dscore_dealt, ALU.mult, ALU.mult)
         nc.scalar.activation(flat(part), flat(root), ACT.Square, accum_out=z[:])
-        nc.vector.reciprocal(rz[:], z[:])
+        grouped0 = grouped_tile("grouped0", 1, "root")
+        group_values(grouped0[:], turned0)
+        part_sq = wide("part_sq", "rows_grouped")
         nc.scalar.activation(flat(part_sq), flat(part), ACT.Square)
-        nc.scalar.activation(flat(weight), flat(part), ACT.Copy, scale=rz[:])
-        quantized_vals = [quantize("vals0", grouped_vals[0][:], P)]
-        grouped_vals.append(gather_values(1))
-        nc.vector.scalar_tensor_tensor(flat(dpart), flat(slope), rz[:], flat(part_sq), ALU.mult, ALU.mult, accum_out=c[:])
-        nc.vector.scalar_tensor_tensor(flat(dweight), flat(weight), c[:], flat(dpart), ALU.mult, ALU.subtract)
-        quantized_vals.append(quantize("vals1", grouped_vals[1][:], P))
-        turned_w = ps.tile([P, PACK, Q], F32, name="turned_w")
-        for t in range(PACK):
-            nc.tensor.transpose(turned_w[:, t, :], dweight[:, t, :], identity[:])
-        grouped_vals.append(gather_values(2))
-        w_grouped = sb.tile([P, Q, PACK], BF16, name="w_grouped", align_bytes=64)
+        turned1 = gather_values(1, "gap", "bank1")
+        nc.vector.tensor_scalar(nz[:], z[:], -1.0, None, ALU.mult)
+        nc.vector.reciprocal(nrz[:], nz[:])
+        nc.scalar.activation(flat(weight), flat(part), ACT.Copy, scale=nrz[:])
+        nc.vector.scalar_tensor_tensor(flat(dpart), flat(slope), nrz[:], flat(part_sq), ALU.mult, ALU.mult, accum_out=c[:])
+        quantized0 = quantize("vals0", grouped0[:], P, "rows_grouped")
+        nc.scalar.activation(flat(shift), flat(weight), ACT.Copy, scale=c[:])
+        turned_w = ps.tile([P, PACK, Q], F32, name="turned_w", tag="score")
+        for term in (dpart, shift):
+            for t in range(PACK):
+                nc.tensor.matmul(
+                    turned_w[:, t, :],
+                    term[:, t, :],
+                    identity[:],
+                    is_transpose=True,
+                    start=(term is dpart and t == 0),
+                    stop=(term is shift and t == PACK - 1),
+                )
+        grouped12 = grouped_tile("grouped12", 2, "weight")
+        group_values(grouped12[:, : P * PACK], turned1)
+        turned2 = gather_values(2, "root", "bank2")
+        group_values(grouped12[:, P * PACK :], turned2)
+        turned3 = gather_values(3, pool_tags[2], "bank1")
+        grouped3 = grouped_tile("grouped3", 1, "grouped3")
+        group_values(grouped3[:], turned3)
+        w_grouped = sb.tile([P, Q, PACK], BF16, name="w_grouped", tag=pool_tags[3], align_bytes=64)
         nc.vector.tensor_tensor(
             w_grouped[:],
             turned_w[:].rearrange("p t q -> p q t"),
             factor_cols[:].unsqueeze(1).to_broadcast([P, Q, PACK]),
             ALU.mult,
         )
-        quantized_vals.append(quantize("vals2", grouped_vals[2][:], P))
+        quantized12 = quantize("vals12", grouped12[:], 2 * P, "factor_cols")
         w_codes, w_scales = quantize("w", w_grouped[:].rearrange("p q t -> p (q t)"), Q)
-        grouped_vals.append(gather_values(3))
-        quantized_vals.append(quantize("vals3", grouped_vals[3][:], P))
+        quantized3 = quantize("vals3", grouped3[:], P, "weight")
 
-        early = ps.tile([P, (BLOCKS - 1) * P], F32, name="early")
-        late = ps.tile([P, P], F32, name="late")
-        for j in range(BLOCKS):
-            codes, scales = quantized_vals[j]
-            nc.tensor.matmul_mx(
-                out=early[:, j * P : (j + 1) * P] if j < BLOCKS - 1 else late[:],
-                lhsT=w_codes[:].bitcast(FP8X4),
-                lhsT_scale=w_scales[:],
-                rhs=codes[:].bitcast(FP8X4),
-                rhs_scale=scales[:],
-                start=True,
-                stop=True,
-            )
-        early_out = sb.tile([P, (BLOCKS - 1) * P], F32, name="early_out")
-        late_out = sb.tile([P, P], F32, name="late_out")
-        nc.scalar.copy(early_out[:], early[:])
-        nc.sync.dma_start(out[:, : (BLOCKS - 1) * P], early_out[:])
-        nc.vector.tensor_copy(late_out[:], late[:])
-        nc.sync.dma_start(out[:, (BLOCKS - 1) * P :], late_out[:])
+        first = 0
+        for name, operands, width, copy, queue in (
+            ("early", (quantized0, quantized12), 3 * P, nc.scalar.copy, nc.scalar),
+            ("late", (quantized3,), P, nc.vector.tensor_copy, nc.sync),
+        ):
+            acc = ps.tile([P, width], F32, name=name)
+            at = 0
+            for codes, scales in operands:
+                n = codes.shape[1]
+                nc.tensor.matmul_mx(
+                    out=acc[:, at : at + n],
+                    lhsT=w_codes[:].bitcast(FP8X4),
+                    lhsT_scale=w_scales[:],
+                    rhs=codes[:].bitcast(FP8X4),
+                    rhs_scale=scales[:],
+                    start=True,
+                    stop=True,
+                )
+                at = at + n
+            result = sb.tile([P, width], F32, name=name + "_out")
+            copy(result[:], acc[:])
+            queue.dma_start(out[:, first : first + width], result[:])
+            first = first + width

from contextlib import ExitStack

import concourse.mybir as mybir
from concourse.masks import make_identity

D, E, T, I, Q = 512, 512, 2048, 512, 128
FLOPS = 2 * (2 * D * Q * I + I * Q * E)

F32 = mybir.dt.float32
BF16 = mybir.dt.bfloat16
I32 = mybir.dt.int32
U32 = mybir.dt.uint32
U16 = mybir.dt.uint16
U8 = mybir.dt.uint8
FP8X4 = mybir.dt.float8_e4m3fn_x4
FP4X4 = mybir.dt.float4_e2m1fn_x4
ACT = mybir.ActivationFunctionType
ALU = mybir.AluOpType

P = 128
PACK = 4
BLOCKS = E // P


def tile_attend_ttnearpoint_kernel(tc, query, keys_words, keys_scales, aim, soft, dquery, slot_factor, vals, offs, out):
    nc = tc.nc
    with ExitStack() as ctx:
        sb = ctx.enter_context(tc.tile_pool(name="sb", bufs=1))
        ps = ctx.enter_context(tc.psum_pool(name="ps", bufs=1))

        offsets = sb.tile([P, I // 16], U16, name="offsets")
        nc.sync.dma_start(offsets[:], offs)

        key_words = sb.tile([P, T], U16, name="key_words", tag="key_words", align_bytes=64)
        nc.sync.dma_start(key_words[:].bitcast(I32), keys_words[0].bitcast(I32))
        query_raw = sb.tile([P, PACK, Q], F32, name="query_raw", tag="query_raw", align_bytes=64)
        nc.sync.dma_start(query_raw[:], query.rearrange("(p t) q -> p t q", t=PACK))
        key_scales = sb.tile([P, T], U8, name="key_scales", tag="key_scales", align_bytes=64)
        nc.gpsimd.memset(key_scales[:, : T // 2].bitcast(I32), 0)
        nc.vector.memset(key_scales[:, T // 2 :].bitcast(I32), 0)
        for r in range(4):
            nc.sync.dma_start(key_scales[r:P:32, :].bitcast(I32), keys_scales[0, r:16:4, :].bitcast(I32))
        dquery_raw = sb.tile([P, PACK, Q], F32, name="dquery_raw", tag="dquery_raw", align_bytes=64)
        nc.sync.dma_start(dquery_raw[:], dquery.rearrange("(p t) q -> p t q", t=PACK))

        warm_in = sb.tile([P, 1], F32, name="warm_in", tag="warm_in", align_bytes=64)
        warm_out = sb.tile([P, 1], F32, name="warm_out")
        nc.vector.memset(warm_in[:], 1.0)
        nc.scalar.activation(warm_out[:], warm_in[:], ACT.Abs_reciprocal_sqrt)

        aim_col = sb.tile([P, 1], F32, name="aim_col")
        soft_col = sb.tile([P, 1], F32, name="soft_col")
        factor_cols = sb.tile([P, PACK], F32, name="factor_cols", tag="factor_cols", align_bytes=64)
        nc.gpsimd.dma_start(aim_col[:], aim)
        nc.gpsimd.dma_start(soft_col[:], soft)
        nc.gpsimd.dma_start(factor_cols[:], slot_factor.rearrange("o (p t) -> (o p) t", t=PACK))
        identity = sb.tile([P, P], F32, name="identity")
        make_identity(nc, identity[:])

        pool_tags = ("warm_in", "key_words", "key_scales", "warm_in")

        def load_values(j):
            val_pool = sb.tile([P, T], F32, name="val_pool%d" % j, tag=pool_tags[j], align_bytes=64)
            nc.sync.dma_start(val_pool[:], vals[j * P : (j + 1) * P, :])
            return val_pool

        def quantize(name, grouped, width, tag=""):
            codes = sb.tile([P, width], U32, name=name + "_codes", tag=tag, align_bytes=64)
            scales = sb.tile([P, width], U8, name=name + "_scales", align_bytes=64)
            nc.vector.quantize_mx(out=codes[:].bitcast(FP8X4), scales=scales[:], in_=grouped)
            return codes, scales

        picked_scales = sb.tile([P, I], U8, name="picked_scales", align_bytes=64)
        picked_words = sb.tile([P, I], U16, name="picked_words", align_bytes=64)
        rows_grouped = sb.tile([P, 2 * Q * PACK], BF16, name="rows_grouped", tag="rows_grouped", align_bytes=64)
        nc.vector.tensor_copy(picked_words[:], key_words[:].indirect(offsets[:]))
        nc.vector.tensor_copy(picked_scales[:], key_scales[:].indirect(offsets[:]))
        for n, raw in enumerate((query_raw, dquery_raw)):
            nc.scalar.copy(
                rows_grouped[:, n * Q * PACK : (n + 1) * Q * PACK].rearrange("p (q t) -> p q t", t=PACK),
                raw[:].rearrange("p t q -> p q t"),
            )
        val_pools = [load_values(j) for j in range(BLOCKS - 1)]
        rows_codes, rows_scales = quantize("rows", rows_grouped[:], 2 * Q)

        score = ps.tile([P, I], F32, name="score", tag="score")
        dscore = ps.tile([P, I], F32, name="dscore")
        for n, acc in enumerate((score, dscore)):
            nc.tensor.matmul_mx(
                out=acc[:],
                lhsT=rows_codes[:, n * Q : (n + 1) * Q].bitcast(FP8X4),
                lhsT_scale=rows_scales[:, n * Q : (n + 1) * Q],
                rhs=picked_words[:].bitcast(FP4X4),
                rhs_scale=picked_scales[:],
                start=True,
                stop=True,
            )

        def gather_values(j, tag, bank):
            picked = sb.tile([P, I], BF16, name="picked_vals%d" % j, tag=tag, align_bytes=64)
            nc.vector.tensor_copy(picked[:], val_pools[j][:].indirect(offsets[:]))
            pairs = picked[:].bitcast(F32)
            turned = ps.tile([P, 2, P], F32, name="turned_vals%d" % j, tag=bank)
            for u in range(2):
                nc.tensor.transpose(turned[:, u, :], pairs[:, u::2], identity[:])
            return turned

        def grouped_tile(name, blocks, tag):
            return sb.tile([P, blocks * P * PACK], BF16, name=name, tag=tag, align_bytes=64)

        def group_values(grouped, turned):
            nc.scalar.copy(
                grouped.bitcast(F32).rearrange("p (e u) -> p e u", u=2),
                turned[:].rearrange("p u e -> p e u"),
            )

        def wide(name, tag=""):
            return sb.tile([P, PACK, P], F32, name=name, tag=tag or name, align_bytes=64)

        def col(name):
            return sb.tile([P, 1], F32, name=name, tag=name, align_bytes=64)

        def flat(t):
            return t[:].rearrange("q t s -> q (t s)")

        score_dealt = score[:].rearrange("q (s t) -> q t s", t=PACK)
        dscore_dealt = dscore[:].rearrange("q (s t) -> q t s", t=PACK)
        gap_sq, gap, root, part, weight, shift, slope, dpart = [
            wide(n) for n in ("gap_sq", "gap", "root", "part", "weight", "shift", "slope", "dpart")
        ]
        z, nz, nrz, c = col("z"), col("nz"), col("nrz"), col("c")

        turned0 = gather_values(0, "rows_grouped", "bank0")
        val_pools.append(load_values(3))
        nc.scalar.activation(gap_sq[:], score_dealt, ACT.Square, bias=aim_col[:], scale=-1.0)
        nc.scalar.activation(gap[:], score_dealt, ACT.Identity, bias=aim_col[:], scale=-1.0)
        nc.scalar.activation(flat(root), flat(gap_sq), ACT.Abs_reciprocal_sqrt, bias=soft_col[:])
        nc.vector.scalar_tensor_tensor(slope[:], gap[:], -2.0, dscore_dealt, ALU.mult, ALU.mult)
        nc.scalar.activation(flat(part), flat(root), ACT.Square, accum_out=z[:])
        grouped0 = grouped_tile("grouped0", 1, "root")
        group_values(grouped0[:], turned0)
        part_sq = wide("part_sq", "rows_grouped")
        nc.scalar.activation(flat(part_sq), flat(part), ACT.Square)
        turned1 = gather_values(1, "gap", "bank1")
        nc.vector.tensor_scalar(nz[:], z[:], -1.0, None, ALU.mult)
        nc.vector.reciprocal(nrz[:], nz[:])
        nc.scalar.activation(flat(weight), flat(part), ACT.Copy, scale=nrz[:])
        nc.vector.scalar_tensor_tensor(flat(dpart), flat(slope), nrz[:], flat(part_sq), ALU.mult, ALU.mult, accum_out=c[:])
        quantized0 = quantize("vals0", grouped0[:], P, "rows_grouped")
        nc.scalar.activation(flat(shift), flat(weight), ACT.Copy, scale=c[:])
        turned_w = ps.tile([P, PACK, Q], F32, name="turned_w", tag="score")
        for term in (dpart, shift):
            for t in range(PACK):
                nc.tensor.matmul(
                    turned_w[:, t, :],
                    term[:, t, :],
                    identity[:],
                    is_transpose=True,
                    start=(term is dpart and t == 0),
                    stop=(term is shift and t == PACK - 1),
                )
        grouped12 = grouped_tile("grouped12", 2, "weight")
        group_values(grouped12[:, : P * PACK], turned1)
        turned2 = gather_values(2, "root", "bank2")
        group_values(grouped12[:, P * PACK :], turned2)
        turned3 = gather_values(3, pool_tags[2], "bank1")
        grouped3 = grouped_tile("grouped3", 1, "grouped3")
        group_values(grouped3[:], turned3)
        w_grouped = sb.tile([P, Q, PACK], BF16, name="w_grouped", tag=pool_tags[3], align_bytes=64)
        nc.vector.tensor_tensor(
            w_grouped[:],
            turned_w[:].rearrange("p t q -> p q t"),
            factor_cols[:].unsqueeze(1).to_broadcast([P, Q, PACK]),
            ALU.mult,
        )
        quantized12 = quantize("vals12", grouped12[:], 2 * P, "factor_cols")
        w_codes, w_scales = quantize("w", w_grouped[:].rearrange("p q t -> p (q t)"), Q)
        quantized3 = quantize("vals3", grouped3[:], P, "weight")

        first = 0
        for name, operands, width, copy, queue in (
            ("early", (quantized0, quantized12), 3 * P, nc.scalar.copy, nc.scalar),
            ("late", (quantized3,), P, nc.vector.tensor_copy, nc.sync),
        ):
            acc = ps.tile([P, width], F32, name=name)
            at = 0
            for codes, scales in operands:
                n = codes.shape[1]
                nc.tensor.matmul_mx(
                    out=acc[:, at : at + n],
                    lhsT=w_codes[:].bitcast(FP8X4),
                    lhsT_scale=w_scales[:],
                    rhs=codes[:].bitcast(FP8X4),
                    rhs_scale=scales[:],
                    start=True,
                    stop=True,
                )
                at = at + n
            result = sb.tile([P, width], F32, name=name + "_out")
            copy(result[:], acc[:])
            queue.dma_start(out[:, first : first + width], result[:])
            first = first + width
